import numpy as np
import ml_dtypes


def mxq(x, axis, fmt="e4m3"):
    dtype, down = {"e4m3": (ml_dtypes.float8_e4m3fn, 7), "e5m2": (ml_dtypes.float8_e5m2, 14)}[fmt]
    v = np.moveaxis(np.asarray(x, np.float32).astype(ml_dtypes.bfloat16).astype(np.float64), axis, -1)
    blocks = v.reshape(v.shape[:-1] + (-1, 32))
    amax = np.abs(blocks).max(-1, keepdims=True)
    byte = np.maximum(np.where(amax > 0, np.frexp(amax)[1] - 1 + 127, 0) - down, 1)
    scale = np.exp2(byte - 127.0)
    codes = (blocks / scale).astype(np.float32).astype(dtype).astype(np.float64)
    return np.moveaxis((codes * scale).reshape(v.shape), -1, axis)


WIDE = False


def mx_kscale(k):
    if not WIDE:
        return np.ones(k)
    levels = np.array([10, -10, 5, -5, 0])
    if k % 512:
        return np.exp2(np.random.permutation(np.resize(levels, k // 32))).repeat(32)
    a = np.empty((k // 512, 16))
    for p in range(k // 512):
        a[p, :8] = np.random.permutation(np.resize(levels, 8))
        for g in range(8):
            far = levels[np.abs(levels - a[p, g]) >= 10]
            a[p, g + 8] = far[np.random.randint(len(far))]
    return np.exp2(a.ravel()).repeat(32)


BF16 = ml_dtypes.bfloat16


def bf(x):
    return np.asarray(x, np.float32).astype(BF16)


def f64(x):
    return np.asarray(x).astype(np.float64)


E2M1 = np.array([0.0, 0.5, 1.0, 1.5, 2.0, 3.0, 4.0, 6.0, -0.0, -0.5, -1.0, -1.5, -2.0, -3.0, -4.0, -6.0])


def pack_weight(w, fmt):
    k, n = w.shape
    w = f64(bf(w)).reshape(k // 32, 32, n)
    amax = np.abs(w).max(1)
    if fmt == "e4m3":
        byte = np.frexp(amax)[1] - 1 + 127 - 7
    else:
        mant, ex = np.frexp(amax / 6.0)
        byte = np.where(mant > 0.5, ex, ex - 1) + 127
    byte = np.clip(np.where(amax > 0, byte, 1), 1, 254)
    scaled = (w * np.exp2(127.0 - byte)[:, None, :]).reshape(k, n).astype(np.float32)
    by_word = np.ascontiguousarray(scaled.reshape(k // 512, 128, 4, n).transpose(0, 1, 3, 2))
    if fmt == "e4m3":
        words = by_word.astype(ml_dtypes.float8_e4m3fn).view(np.uint8)
    else:
        c = by_word.astype(ml_dtypes.float4_e2m1fn).view(np.uint8) & 0xF
        words = c[..., 0::2] | (c[..., 1::2] << 4)
    return np.ascontiguousarray(words), np.ascontiguousarray(byte.astype(np.uint8).reshape(k // 512, 16, n))


def unpack_weight(words, scales, fmt):
    g, p, n, _ = words.shape
    if fmt == "e4m3":
        vals = np.ascontiguousarray(words).view(ml_dtypes.float8_e4m3fn).astype(np.float64)
    else:
        nib = np.empty((g, p, n, 4), np.uint8)
        nib[..., 0::2] = words & 0xF
        nib[..., 1::2] = words >> 4
        vals = E2M1[nib]
    vals = vals * np.repeat(np.exp2(scales.astype(np.float64) - 127.0), 8, axis=1)[..., None]
    return vals.transpose(0, 1, 3, 2).reshape(g * 512, n)

def planes(Y):
    n, m = Y.shape
    b = f64(bf(Y)).reshape(n // 32, 32, m)
    amax = np.abs(b).max(1)
    byte = np.clip(np.where(amax > 0, np.frexp(amax)[1] - 1 + 127 - 7, 1), 1, 254)
    codes = (b * np.exp2(127.0 - byte)[:, None, :]).reshape(n, m).astype(np.float32).astype(ml_dtypes.float8_e4m3fn).view(np.uint8)
    words = codes.reshape(n // 512, 128, 4, m).transpose(0, 1, 3, 2)
    return np.ascontiguousarray(words), np.ascontiguousarray(byte.astype(np.uint8).reshape(n // 512, 16, m))


B, I, J, N, M = 256, 4, 4, 1024, 1024


def ridge_filter(zc, g):
    num = g * np.sum(zc, axis=1)
    den = np.sum(zc * zc, axis=1) + 1.0
    return num / den


def setup_inputs():
    s, t = mx_kscale(N), mx_kscale(M)
    z = bf(np.random.standard_normal((B, I, N)) * s)
    x = bf(np.random.standard_normal((B, J, N)) * s)
    phi_words, phi_scales = pack_weight(np.random.standard_normal((N, M)) / np.sqrt(N) / s[:, None], "e4m3")
    g = bf(np.random.standard_normal((B, M)) * t)
    psi_words, psi_scales = pack_weight(np.random.standard_normal((M, N)) / np.sqrt(M) / t[:, None], "e4m3")
    return {"z": z,
            "x": x,
            "phi_words": phi_words,
            "phi_scales": phi_scales,
            "g": g,
            "psi_words": psi_words,
            "psi_scales": psi_scales}


def core(z, x, phi_words, phi_scales, g, psi_words, psi_scales):
    phiq = unpack_weight(phi_words, phi_scales, "e4m3")
    zc = mxq(f64(z), 2, "e4m3") @ phiq
    xc = mxq(f64(x), 2, "e4m3") @ phiq
    h = ridge_filter(zc, f64(g))
    return mxq(xc * h[:, None, :], 2, "e4m3") @ unpack_weight(psi_words, psi_scales, "e4m3")


def reference(z, x, phi_words, phi_scales, g, psi_words, psi_scales):
    R_out = core(z, x, phi_words, phi_scales, g, psi_words, psi_scales)
    words, scales = planes(np.moveaxis(R_out, 2, 0).reshape(1024, -1))
    return R_out, words, scales

@@ -1,0 +1,357 @@
+from contextlib import ExitStack
+
+import concourse.mybir as mybir
+from concourse.masks import make_identity
+
+F32 = mybir.dt.float32
+BF16 = mybir.dt.bfloat16
+I32 = mybir.dt.int32
+U32 = mybir.dt.uint32
+U8 = mybir.dt.uint8
+FP8X4 = mybir.dt.float8_e4m3fn_x4
+ADD = mybir.AluOpType.add
+MULT = mybir.AluOpType.mult
+ACT = mybir.ActivationFunctionType
+AXIS_X = mybir.AxisListType.X
+
+B, T, K = 256, 4, 1024
+ROWS = B * T
+FLOPS = 3 * 2 * ROWS * K * K
+P = 128
+GROUPS = K // 512
+UNIT = 256
+UB = UNIT // T
+UNITS = ROWS // UNIT
+RT = UNIT // P
+
+
+def tile_learnedbasisridgecorrelationfilter_x2_kernel(
+    tc, z, x, phi_words, phi_scales, g, psi_words, psi_scales, out_0, out_1, out_2
+):
+    nc = tc.nc
+    z_rows = z.flatten_outer_dims()
+    x_rows = x.flatten_outer_dims()
+    out_rows = out_0.flatten_outer_dims()
+
+    with ExitStack() as ctx:
+        keep = ctx.enter_context(tc.tile_pool(name="keep", bufs=1))
+        work = ctx.enter_context(tc.tile_pool(name="work", bufs=2))
+        psum = ctx.enter_context(tc.psum_pool(name="psum", bufs=1))
+
+        ident = keep.tile([P, P], F32, name="ident")
+        make_identity(nc, ident[:])
+        ctx.enter_context(tc.manual_schedule())
+
+        warm = keep.tile([P, 1], F32, name="warm")
+        nc.vector.memset(warm[:], 1.0)
+        warm_out = keep.tile([P, 1], F32, name="warm_out")
+        nc.scalar.activation(out=warm_out[:], in_=warm[:], func=ACT.Abs_reciprocal_sqrt)
+        phi_s = keep.tile([P, K], U8, name="phi_s", align_bytes=64)
+        psi_s = keep.tile([P, K], U8, name="psi_s", align_bytes=64)
+        nc.vector.memset(phi_s[:].bitcast(I32), 0)
+        nc.vector.memset(psi_s[:].bitcast(I32), 0)
+
+        def load_rows(rows, u, name):
+            t = keep.tile([P, RT, K], BF16, name="%s%d" % (name, u), align_bytes=64)
+            nc.sync.dma_start(
+                out=t[:],
+                in_=rows[UNIT * u : UNIT * (u + 1), :].rearrange("(s p) k -> p s k", p=P),
+            )
+            return t
+
+        def load_scales(plane, scales):
+            for q in range(4):
+                nc.sync.dma_start(
+                    out=plane[32 * q : 32 * q + 8, :].bitcast(I32),
+                    in_=scales[:, 4 * q : 4 * q + 4, :].bitcast(I32),
+                )
+
+        phi_raw = [keep.tile([P, GROUPS, 512], I32, name="phi_raw%d" % h, align_bytes=64) for h in range(2)]
+        phi_p = [keep.tile([P, GROUPS, 4, P], I32, name="phi_p%d" % h, align_bytes=64) for h in range(2)]
+        phi_sp = keep.tile([P, 2, 4, P], U8, name="phi_sp", align_bytes=64)
+        psi_w = keep.tile([P, GROUPS, K], I32, name="psi_w", align_bytes=64)
+        g_in = keep.tile([P, 2, K], BF16, name="g_in", align_bytes=64)
+        g_t = keep.tile([P, GROUPS, 2, B], F32, name="g_t", align_bytes=64)
+
+        def load_phi(h):
+            nc.sync.dma_start(
+                out=phi_raw[h][:],
+                in_=phi_words[:, :, 512 * h : 512 * (h + 1), :].rearrange("g p n t -> p g (n t)").bitcast(I32),
+            )
+
+        z_in, x_in = [], []
+        z_in.append(load_rows(z_rows, 0, "z"))
+        load_scales(phi_s, phi_scales)
+        load_phi(0)
+        load_phi(1)
+        x_in.append(load_rows(x_rows, 0, "x"))
+        z_in.append(load_rows(z_rows, 1, "z"))
+        nc.sync.dma_start(out=g_in[:], in_=g.rearrange("(s p) k -> p s k", p=P))
+        x_in.append(load_rows(x_rows, 1, "x"))
+        z_in.append(load_rows(z_rows, 2, "z"))
+        load_scales(psi_s, psi_scales)
+        nc.sync.dma_start(out=psi_w[:], in_=psi_words.rearrange("g p n t -> p g (n t)").bitcast(I32))
+        x_in.append(load_rows(x_rows, 2, "x"))
+        z_in.append(load_rows(z_rows, 3, "z"))
+        x_in.append(load_rows(x_rows, 3, "x"))
+
+        def permute_phi(h):
+            nc.vector.tensor_copy(
+                out=phi_p[h][:], in_=phi_raw[h][:].rearrange("p g (m t) -> p g t m", t=4)
+            )
+
+        def turn(t_in, name):
+            words = t_in[:].rearrange("p s k -> p (s k)").bitcast(F32)
+            turned = work.tile([P, GROUPS, UNIT, 4], BF16, name="turned_" + name, tag="turned", bufs=3, align_bytes=64)
+            for gr in range(GROUPS):
+                bank = psum.tile([P, 2, UNIT], F32, name="bank_t", tag="tp", bufs=2)
+                for e in range(2):
+                    for s in range(RT):
+                        first = 512 * s + 256 * gr
+                        nc.tensor.transpose(
+                            bank[:, e, P * s : P * (s + 1)], words[:, first + e : first + 256 : 2], ident[:]
+                        )
+                nc.scalar.copy(
+                    out=turned[:, gr].rearrange("p r j -> p (r j)").bitcast(F32).rearrange("p (r e) -> p r e", e=2),
+                    in_=bank[:].rearrange("p e r -> p r e"),
+                )
+            return turned
+
+        def quantize(turned, name):
+            codes = work.tile([P, GROUPS, UNIT], U32, name="codes_" + name, tag="codes_" + name, bufs=2, align_bytes=64)
+            scales = work.tile([P, GROUPS, UNIT], U8, name="scales_" + name, tag="scales_" + name, bufs=2, align_bytes=64)
+            nc.vector.quantize_mx(
+                out=codes[:].rearrange("p g r -> p (g r)").bitcast(FP8X4),
+                scales=scales[:].rearrange("p g r -> p (g r)"),
+                in_=turned[:].rearrange("p g r j -> p (g r j)"),
+            )
+            return codes, scales
+
+        def turn_g():
+            words = g_in[:].rearrange("p s k -> p (s k)").bitcast(F32)
+            for gr in range(GROUPS):
+                bank = psum.tile([P, 2, B], F32, name="bank_g", tag="tp", bufs=2)
+                for e in range(2):
+                    for s in range(2):
+                        first = 512 * s + 256 * gr
+                        nc.tensor.transpose(
+                            bank[:, e, P * s : P * (s + 1)], words[:, first + e : first + 256 : 2], ident[:]
+                        )
+                nc.scalar.copy(out=g_t[:, gr], in_=bank[:])
+
+        def z_stage(zq, u):
+            codes, scales = zq
+            squares = work.tile([P, 4, 512], F32, name="squares")
+            sums = work.tile([P, 8, UB], F32, name="sums")
+            for h in range(2):
+                for tp in range(2):
+                    bank = psum.tile([P, 2, UNIT], F32, name="bank_z", tag="mm", bufs=6)
+                    for ti in range(2):
+                        for gr in range(GROUPS):
+                            nc.tensor.matmul_mx(
+                                out=bank[:, ti, :],
+                                lhsT=phi_p[h][:, gr, 2 * tp + ti, :].bitcast(FP8X4),
+                                lhsT_scale=phi_sp[4 * gr : P, h, 2 * tp + ti, :],
+                                rhs=codes[:, gr, :].bitcast(FP8X4),
+                                rhs_scale=scales[:, gr, :],
+                                start=(gr == 0),
+                                stop=(gr == GROUPS - 1),
+                            )
+                    n = 2 * h + tp
+                    nc.scalar.activation(
+                        out=squares[:, n, :], in_=bank[:].rearrange("p t r -> p (t r)"), func=ACT.Square
+                    )
+                    nc.vector.tensor_reduce(
+                        out=sums[:, 2 * n : 2 * n + 2, :],
+                        in_=bank[:].rearrange("p t (b i) -> p t b i", i=T),
+                        axis=AXIS_X,
+                        op=ADD,
+                    )
+            return squares, sums
+
+        def pair_sums(squares):
+            pairs = work.tile([P, 8 * UB, 2], F32, name="pairs")
+            sq = squares[:].rearrange("p n (b i) -> p (n b) i", i=T)
+            nc.gpsimd.tensor_tensor(out=pairs[:], in0=sq[:, :, 0:2], in1=sq[:, :, 2:4], op=ADD)
+            return pairs
+
+        def filter_den(pairs):
+            den = work.tile([P, 8 * UB], F32, name="den")
+            nc.vector.tensor_tensor(out=den[:], in0=pairs[:, :, 0], in1=pairs[:, :, 1], op=ADD)
+            root = work.tile([P, 8 * UB], F32, name="root")
+            nc.scalar.activation(out=root[:], in_=den[:], func=ACT.Abs_reciprocal_sqrt, bias=1.0)
+            inv = work.tile([P, 8 * UB], F32, name="inv")
+            nc.scalar.activation(out=inv[:], in_=root[:], func=ACT.Square)
+            return inv
+
+        def filter_num(sums, u):
+            num = work.tile([P, 8, UB], F32, name="num")
+            g_view = g_t[:].rearrange("p g e b -> p (g e b)").bitcast(BF16)
+            g_view = g_view.rearrange("p (k b v) -> p k v b", k=4, v=2)
+            nc.vector.tensor_tensor(
+                out=num[:].rearrange("p (k v) b -> p k v b", v=2),
+                in0=sums[:].rearrange("p (k v) b -> p k v b", v=2),
+                in1=g_view[:, :, :, UB * u : UB * (u + 1)],
+                op=MULT,
+            )
+            return num
+
+        def filter_h(num, inv):
+            filt = work.tile([P, 8, UB], F32, name="filt")
+            nc.vector.tensor_tensor(
+                out=filt[:].rearrange("p n b -> p (n b)"),
+                in0=num[:].rearrange("p n b -> p (n b)"),
+                in1=inv[:],
+                op=MULT,
+            )
+            return filt
+
+        def x_stage(xq, filt):
+            codes, scales = xq
+            ys = []
+            for rt in range(RT):
+                y = work.tile([P, GROUPS, P, 4], BF16, name="y", bufs=3, align_bytes=64)
+                nb = P // T
+                for h in range(2):
+                    bank = psum.tile([P, 4, P], F32, name="bank_x", tag="mm", bufs=6)
+                    for t in range(4):
+                        for gr in range(GROUPS):
+                            nc.tensor.matmul_mx(
+                                out=bank[:, t, :],
+                                lhsT=phi_p[h][:, gr, t, :].bitcast(FP8X4),
+                                lhsT_scale=phi_sp[4 * gr : P, h, t, :],
+                                rhs=codes[:, gr, P * rt : P * (rt + 1)].bitcast(FP8X4),
+                                rhs_scale=scales[:, gr, P * rt : P * (rt + 1)],
+                                start=(gr == 0),
+                                stop=(gr == GROUPS - 1),
+                            )
+                    f = filt[:, 4 * h : 4 * h + 4, nb * rt : nb * (rt + 1)].rearrange("p t b -> p b t")
+                    nc.vector.tensor_tensor(
+                        out=y[:, h].rearrange("p (b j) t -> p b j t", j=T),
+                        in0=bank[:].rearrange("p t (b j) -> p b j t", j=T),
+                        in1=f.unsqueeze(2).to_broadcast([P, nb, T, 4]),
+                        op=MULT,
+                    )
+                ys.append(y)
+            return ys
+
+        def quantize_y(ys):
+            res = []
+            for y in ys:
+                codes = work.tile([P, GROUPS, P], U32, name="y_codes", bufs=3, align_bytes=64)
+                scales = work.tile([P, GROUPS, P], U8, name="y_scales", bufs=3, align_bytes=64)
+                nc.vector.quantize_mx(
+                    out=codes[:].rearrange("p g r -> p (g r)").bitcast(FP8X4),
+                    scales=scales[:].rearrange("p g r -> p (g r)"),
+                    in_=y[:].rearrange("p g r j -> p (g r j)"),
+                )
+                res.append((codes, scales))
+            return res
+
+        def out_stage(yq, u):
+            rounded = []
+            for rt in range(RT):
+                codes, scales = yq[rt]
+                rows = work.tile([P, K], F32, name="rows", bufs=3)
+                short = work.tile([P, K], BF16, name="short", bufs=4, align_bytes=64)
+                for h in range(2):
+                    bank = psum.tile([P, 512], F32, name="bank_o", tag="mm", bufs=6)
+                    cols = slice(512 * h, 512 * (h + 1))
+                    for gr in range(GROUPS):
+                        nc.tensor.matmul_mx(
+                            out=bank[:],
+                            lhsT=codes[:, gr, :].bitcast(FP8X4),
+                            lhsT_scale=scales[:, gr, :],
+                            rhs=psi_w[:, gr, cols].bitcast(FP8X4),
+                            rhs_scale=psi_s[4 * gr : P, cols],
+                            start=(gr == 0),
+                            stop=(gr == GROUPS - 1),
+                        )
+                    nc.scalar.copy(out=rows[:, cols], in_=bank[:])
+                    nc.gpsimd.tensor_scalar(
+                        out=short[:, cols].rearrange("p (e q v) -> p e q v", e=2, v=2),
+                        in0=rows[:, cols].rearrange("p (q e v) -> p e q v", e=2, v=2),
+                        scalar1=1.0,
+                        scalar2=0.0,
+                        op0=MULT,
+                        op1=ADD,
+                    )
+                r0 = UNIT * u + P * rt
+                nc.sync.dma_start(out=out_rows[r0 : r0 + P, :], in_=rows[:])
+                rounded.append(short)
+            return rounded
+
+        def plane_stage(rounded, u):
+            turned = work.tile([P, GROUPS, UNIT, 4], BF16, name="turned_o", tag="turned", bufs=3, align_bytes=64)
+            for gr in range(GROUPS):
+                bank = psum.tile([P, 2, UNIT], F32, name="bank_p", tag="tp", bufs=2)
+                for rt in range(RT):
+                    words = rounded[rt][:].bitcast(F32)
+                    for e in range(2):
+                        first = 256 * gr + 128 * e
+                        nc.tensor.transpose(bank[:, e, P * rt : P * (rt + 1)], words[:, first : first + P], ident[:])
+                nc.scalar.copy(
+                    out=turned[:, gr].rearrange("p r j -> p (r j)").bitcast(F32).rearrange("p (r e) -> p r e", e=2),
+                    in_=bank[:].rearrange("p e r -> p r e"),
+                )
+            codes = work.tile([P, GROUPS, UNIT], U32, name="o_codes", align_bytes=64)
+            scales = work.tile([P, GROUPS * UNIT], U8, name="o_scales", align_bytes=64)
+            nc.vector.quantize_mx(
+                out=codes[:].rearrange("p g r -> p (g r)").bitcast(FP8X4),
+                scales=scales[:],
+                in_=turned[:].rearrange("p g r j -> p (g r j)"),
+            )
+            cols = slice(UNIT * u, UNIT * (u + 1))
+            nc.sync.dma_start(
+                out=out_1[:, :, cols, :].rearrange("g p m t -> p g (m t)").bitcast(I32), in_=codes[:].bitcast(I32)
+            )
+            for q in range(4):
+                nc.sync.dma_start(
+                    out=out_2[:, 4 * q : 4 * q + 4, cols].bitcast(I32).rearrange("g r m -> r g m"),
+                    in_=scales[32 * q : 32 * q + 4, :].bitcast(I32).rearrange("r (g m) -> r g m", g=GROUPS),
+                )
+
+        zq, xq, zs, num, inv, filt, yq, short = {}, {}, {}, {}, {}, {}, {}, {}
+        zt = turn(z_in[0], "z")
+        permute_phi(0)
+        zq[0] = quantize(zt, "z")
+        nc.vector.tensor_copy(
+            out=phi_sp[:],
+            in_=phi_s[:].rearrange("p (h m t) -> p h t m", h=2, t=4),
+        )
+        permute_phi(1)
+        zs[0] = z_stage(zq[0], 0)
+        pairs = pair_sums(zs[0][0])
+        xt = turn(x_in[0], "x")
+        xq[0] = quantize(xt, "x")
+        zt = turn(z_in[1], "z")
+        inv[0] = filter_den(pairs)
+        zq[1] = quantize(zt, "z")
+        turn_g()
+        num[0] = filter_num(zs[0][1], 0)
+        filt[0] = filter_h(num[0], inv[0])
+
+        for k in range(UNITS):
+            if k + 1 < UNITS:
+                zs[k + 1] = z_stage(zq[k + 1], k + 1)
+                pairs = pair_sums(zs[k + 1][0])
+            if k >= 1:
+                short[k - 1] = out_stage(yq[k - 1], k - 1)
+            if k + 2 < UNITS:
+                zt = turn(z_in[k + 2], "z")
+            if k + 1 < UNITS:
+                inv[k + 1] = filter_den(pairs)
+            ys = x_stage(xq[k], filt[k])
+            if k + 2 < UNITS:
+                zq[k + 2] = quantize(zt, "z")
+            if k + 1 < UNITS:
+                num[k + 1] = filter_num(zs[k + 1][1], k + 1)
+            yq[k] = quantize_y(ys)
+            if k + 1 < UNITS:
+                xt = turn(x_in[k + 1], "x")
+                filt[k + 1] = filter_h(num[k + 1], inv[k + 1])
+                xq[k + 1] = quantize(xt, "x")
+            if k >= 1:
+                plane_stage(short[k - 1], k - 1)
+        short[UNITS - 1] = out_stage(yq[UNITS - 1], UNITS - 1)
+        plane_stage(short[UNITS - 1], UNITS - 1)

@@ -24,18 +24,60 @@ UB = UNIT // T
 UNITS = ROWS // UNIT
 RT = UNIT // P
 
+SHORT_LIVED = ("squares", "pairs", "den", "root", "inv", "num", "turned_o0", "turned_o1")
+SLOT = (
+    ("z_bank", 3, 2),
+    ("pair_squares", 1, 2),
+    ("turn_out", 0, 5),
+    ("x_bank", 2, 3),
+    ("turn_x", 1, 2),
+    ("out_bank", 1, 4),
+    ("quantize_y", 0, 3),
+    ("turn_x", 0, 1),
+    ("out_bank", 2, 4),
+    ("phi_words_of", 1, 1),
+    ("quantize_x", 0, 2),
+    ("sum_squares", 0, 2),
+    ("quantize_out", 0, 5),
+    ("x_bank", 3, 3),
+    ("round_bank", 1, 4),
+    ("out_bank", 3, 4),
+    ("turn_out", 1, 5),
+    ("turn_g", 0, 2),
+    ("numerator", 0, 2),
+    ("z_bank", 0, 1),
+    ("z_bank", 1, 1),
+    ("quantize_y", 1, 3),
+    ("pair_squares", 0, 1),
+    ("out_bank", 0, 3),
+    ("invert", 0, 2),
+    ("round_bank", 2, 4),
+    ("round_bank", 3, 4),
+    ("ridge", 0, 2),
+    ("quantize_out", 1, 5),
+    ("z_bank", 2, 1),
+    ("phi_scales_of", 0, 0),
+    ("turn_z", 0, 0),
+    ("round_bank", 0, 3),
+    ("phi_words_of", 0, 0),
+    ("turn_z", 1, 0),
+    ("x_bank", 0, 2),
+    ("x_bank", 1, 2),
+    ("quantize_z", 0, 0),
+    ("phi_scales_of", 1, 0),
+)
+
 
 def tile_learnedbasisridgecorrelationfilter_x2_kernel(
     tc, z, x, phi_words, phi_scales, g, psi_words, psi_scales, out_0, out_1, out_2
 ):
     nc = tc.nc
-    z_rows = z.flatten_outer_dims()
-    x_rows = x.flatten_outer_dims()
     out_rows = out_0.flatten_outer_dims()
+    in_rows = {"z": z.flatten_outer_dims(), "x": x.flatten_outer_dims()}
 
     with ExitStack() as ctx:
         keep = ctx.enter_context(tc.tile_pool(name="keep", bufs=1))
-        work = ctx.enter_context(tc.tile_pool(name="work", bufs=2))
+        work = ctx.enter_context(tc.tile_pool(name="work", bufs=3))
         psum = ctx.enter_context(tc.psum_pool(name="psum", bufs=1))
 
         ident = keep.tile([P, P], F32, name="ident")
@@ -51,13 +93,23 @@ def tile_learnedbasisridgecorrelationfilter_x2_kernel(
         nc.vector.memset(phi_s[:].bitcast(I32), 0)
         nc.vector.memset(psi_s[:].bitcast(I32), 0)
 
-        def load_rows(rows, u, name):
-            t = keep.tile([P, RT, K], BF16, name="%s%d" % (name, u), align_bytes=64)
-            nc.sync.dma_start(
-                out=t[:],
-                in_=rows[UNIT * u : UNIT * (u + 1), :].rearrange("(s p) k -> p s k", p=P),
-            )
-            return t
+        phi_raw = [keep.tile([P, GROUPS, 512], I32, name="phi_raw%d" % h, align_bytes=64) for h in range(2)]
+        phi_p = [keep.tile([P, GROUPS, 4, P], I32, name="phi_p%d" % h, align_bytes=64) for h in range(2)]
+        phi_sp = [keep.tile([P, 4, P], U8, name="phi_sp%d" % h, align_bytes=64) for h in range(2)]
+        psi_w = keep.tile([P, GROUPS, K], I32, name="psi_w", align_bytes=64)
+        g_in = keep.tile([P, 2, K], BF16, name="g_in", align_bytes=64)
+        g_t = keep.tile([P, 2, GROUPS, 2, P], F32, name="g_t", align_bytes=64)
+        t_in = {}
+
+        def load_rows(src, u, split=1):
+            t = keep.tile([P, RT, K], BF16, name="%s%d" % (src, u), align_bytes=64)
+            for s in range(split):
+                n = RT // split
+                nc.sync.dma_start(
+                    out=t[:, n * s : n * (s + 1), :],
+                    in_=in_rows[src][UNIT * u + P * n * s : UNIT * u + P * n * (s + 1), :].rearrange("(s p) k -> p s k", p=P),
+                )
+            t_in[src, u] = t
 
         def load_scales(plane, scales):
             for q in range(4):
@@ -66,292 +118,265 @@ def tile_learnedbasisridgecorrelationfilter_x2_kernel(
                     in_=scales[:, 4 * q : 4 * q + 4, :].bitcast(I32),
                 )
 
-        phi_raw = [keep.tile([P, GROUPS, 512], I32, name="phi_raw%d" % h, align_bytes=64) for h in range(2)]
-        phi_p = [keep.tile([P, GROUPS, 4, P], I32, name="phi_p%d" % h, align_bytes=64) for h in range(2)]
-        phi_sp = keep.tile([P, 2, 4, P], U8, name="phi_sp", align_bytes=64)
-        psi_w = keep.tile([P, GROUPS, K], I32, name="psi_w", align_bytes=64)
-        g_in = keep.tile([P, 2, K], BF16, name="g_in", align_bytes=64)
-        g_t = keep.tile([P, GROUPS, 2, B], F32, name="g_t", align_bytes=64)
-
         def load_phi(h):
             nc.sync.dma_start(
                 out=phi_raw[h][:],
                 in_=phi_words[:, :, 512 * h : 512 * (h + 1), :].rearrange("g p n t -> p g (n t)").bitcast(I32),
             )
 
-        z_in, x_in = [], []
-        z_in.append(load_rows(z_rows, 0, "z"))
+        load_rows("z", 0, split=2)
         load_scales(phi_s, phi_scales)
         load_phi(0)
+        load_rows("x", 0)
         load_phi(1)
-        x_in.append(load_rows(x_rows, 0, "x"))
-        z_in.append(load_rows(z_rows, 1, "z"))
+        load_rows("z", 1)
         nc.sync.dma_start(out=g_in[:], in_=g.rearrange("(s p) k -> p s k", p=P))
-        x_in.append(load_rows(x_rows, 1, "x"))
-        z_in.append(load_rows(z_rows, 2, "z"))
+        load_rows("x", 1)
         load_scales(psi_s, psi_scales)
         nc.sync.dma_start(out=psi_w[:], in_=psi_words.rearrange("g p n t -> p g (n t)").bitcast(I32))
-        x_in.append(load_rows(x_rows, 2, "x"))
-        z_in.append(load_rows(z_rows, 3, "z"))
-        x_in.append(load_rows(x_rows, 3, "x"))
+        load_rows("z", 2)
+        load_rows("x", 2)
+        load_rows("z", 3)
+        load_rows("x", 3)
 
-        def permute_phi(h):
-            nc.vector.tensor_copy(
-                out=phi_p[h][:], in_=phi_raw[h][:].rearrange("p g (m t) -> p g t m", t=4)
+        tiles = {}
+
+        def tile_of(key, u, shape, dtype):
+            if (key, u) not in tiles:
+                bufs = 2 if key in SHORT_LIVED else 3
+                tiles[key, u] = work.tile(shape, dtype, name=key, tag=key, bufs=bufs, align_bytes=64)
+            return tiles[key, u]
+
+        def phi_words_of(u, h):
+            if u == 0:
+                nc.vector.tensor_copy(out=phi_p[h][:], in_=phi_raw[h][:].rearrange("p g (m t) -> p g t m", t=4))
+
+        def phi_scales_of(u, h):
+            if u == 0:
+                nc.vector.tensor_copy(
+                    out=phi_sp[h][:], in_=phi_s[:, 512 * h : 512 * (h + 1)].rearrange("p (m t) -> p t m", t=4)
+                )
+
+        def bank_to_words(bank, dst):
+            nc.scalar.copy(
+                out=dst.rearrange("p r j -> p (r j)").bitcast(F32).rearrange("p (r e) -> p r e", e=2),
+                in_=bank[:].rearrange("p e r -> p r e"),
             )
 
-        def turn(t_in, name):
-            words = t_in[:].rearrange("p s k -> p (s k)").bitcast(F32)
-            turned = work.tile([P, GROUPS, UNIT, 4], BF16, name="turned_" + name, tag="turned", bufs=3, align_bytes=64)
-            for gr in range(GROUPS):
-                bank = psum.tile([P, 2, UNIT], F32, name="bank_t", tag="tp", bufs=2)
+        def turn(src, u, gr):
+            turned = tile_of("turned_" + src, u, [P, GROUPS, UNIT, 4], BF16)
+            words = t_in[src, u][:].rearrange("p s k -> p (s k)").bitcast(F32)
+            bank = psum.tile([P, 2, UNIT], F32, name="bank_t", tag="tp", bufs=3)
+            for s in range(RT):
                 for e in range(2):
-                    for s in range(RT):
-                        first = 512 * s + 256 * gr
-                        nc.tensor.transpose(
-                            bank[:, e, P * s : P * (s + 1)], words[:, first + e : first + 256 : 2], ident[:]
-                        )
-                nc.scalar.copy(
-                    out=turned[:, gr].rearrange("p r j -> p (r j)").bitcast(F32).rearrange("p (r e) -> p r e", e=2),
-                    in_=bank[:].rearrange("p e r -> p r e"),
-                )
-            return turned
+                    first = 512 * s + 256 * gr
+                    nc.tensor.transpose(bank[:, e, P * s : P * (s + 1)], words[:, first + e : first + 256 : 2], ident[:])
+            bank_to_words(bank, turned[:, gr])
 
-        def quantize(turned, name):
-            codes = work.tile([P, GROUPS, UNIT], U32, name="codes_" + name, tag="codes_" + name, bufs=2, align_bytes=64)
-            scales = work.tile([P, GROUPS, UNIT], U8, name="scales_" + name, tag="scales_" + name, bufs=2, align_bytes=64)
+        def turn_z(u, gr):
+            turn("z", u, gr)
+
+        def turn_x(u, gr):
+            turn("x", u, gr)
+
+        def quantize(key, u, turned, shape):
+            codes = tile_of("codes_" + key, u, shape, U32)
+            scales = tile_of("scales_" + key, u, shape, U8)
             nc.vector.quantize_mx(
                 out=codes[:].rearrange("p g r -> p (g r)").bitcast(FP8X4),
                 scales=scales[:].rearrange("p g r -> p (g r)"),
                 in_=turned[:].rearrange("p g r j -> p (g r j)"),
             )
-            return codes, scales
 
-        def turn_g():
-            words = g_in[:].rearrange("p s k -> p (s k)").bitcast(F32)
-            for gr in range(GROUPS):
-                bank = psum.tile([P, 2, B], F32, name="bank_g", tag="tp", bufs=2)
-                for e in range(2):
-                    for s in range(2):
-                        first = 512 * s + 256 * gr
-                        nc.tensor.transpose(
-                            bank[:, e, P * s : P * (s + 1)], words[:, first + e : first + 256 : 2], ident[:]
-                        )
-                nc.scalar.copy(out=g_t[:, gr], in_=bank[:])
+        def quantize_z(u, i):
+            quantize("z", u, tiles["turned_z", u], [P, GROUPS, UNIT])
 
-        def z_stage(zq, u):
-            codes, scales = zq
-            squares = work.tile([P, 4, 512], F32, name="squares")
-            sums = work.tile([P, 8, UB], F32, name="sums")
-            for h in range(2):
-                for tp in range(2):
-                    bank = psum.tile([P, 2, UNIT], F32, name="bank_z", tag="mm", bufs=6)
-                    for ti in range(2):
-                        for gr in range(GROUPS):
-                            nc.tensor.matmul_mx(
-                                out=bank[:, ti, :],
-                                lhsT=phi_p[h][:, gr, 2 * tp + ti, :].bitcast(FP8X4),
-                                lhsT_scale=phi_sp[4 * gr : P, h, 2 * tp + ti, :],
-                                rhs=codes[:, gr, :].bitcast(FP8X4),
-                                rhs_scale=scales[:, gr, :],
-                                start=(gr == 0),
-                                stop=(gr == GROUPS - 1),
-                            )
-                    n = 2 * h + tp
-                    nc.scalar.activation(
-                        out=squares[:, n, :], in_=bank[:].rearrange("p t r -> p (t r)"), func=ACT.Square
+        def quantize_x(u, i):
+            quantize("x", u, tiles["turned_x", u], [P, GROUPS, UNIT])
+
+        def turn_g(u, i):
+            if u % 2 == 0:
+                s = u // 2
+                words = g_in[:, s, :].bitcast(F32)
+                bank = psum.tile([P, GROUPS, 2, P], F32, name="bank_g", tag="tp", bufs=3)
+                for gr in range(GROUPS):
+                    for e in range(2):
+                        nc.tensor.transpose(bank[:, gr, e, :], words[:, 256 * gr + e : 256 * (gr + 1) : 2], ident[:])
+                nc.scalar.copy(out=g_t[:, s], in_=bank[:])
+
+        def z_bank(u, n):
+            codes, scales = tiles["codes_z", u], tiles["scales_z", u]
+            squares = tile_of("squares", u, [P, 4, 512], F32)
+            sums = tile_of("sums", u, [P, 8, UB], F32)
+            h = n // 2
+            bank = psum.tile([P, 2, UNIT], F32, name="bank_z", tag="mm", bufs=5)
+            for ti in range(2):
+                t = 2 * (n % 2) + ti
+                for gr in range(GROUPS):
+                    nc.tensor.matmul_mx(
+                        out=bank[:, ti, :],
+                        lhsT=phi_p[h][:, gr, t, :].bitcast(FP8X4),
+                        lhsT_scale=phi_sp[h][4 * gr : P, t, :],
+                        rhs=codes[:, gr, :].bitcast(FP8X4),
+                        rhs_scale=scales[:, gr, :],
+                        start=(gr == 0),
+                        stop=(gr == GROUPS - 1),
                     )
-                    nc.vector.tensor_reduce(
-                        out=sums[:, 2 * n : 2 * n + 2, :],
-                        in_=bank[:].rearrange("p t (b i) -> p t b i", i=T),
-                        axis=AXIS_X,
-                        op=ADD,
-                    )
-            return squares, sums
+            nc.scalar.activation(out=squares[:, n, :], in_=bank[:].rearrange("p t r -> p (t r)"), func=ACT.Square)
+            nc.vector.tensor_reduce(
+                out=sums[:, 2 * n : 2 * n + 2, :],
+                in_=bank[:].rearrange("p t (b i) -> p t b i", i=T),
+                axis=AXIS_X,
+                op=ADD,
+            )
 
-        def pair_sums(squares):
-            pairs = work.tile([P, 8 * UB, 2], F32, name="pairs")
-            sq = squares[:].rearrange("p n (b i) -> p (n b) i", i=T)
-            nc.gpsimd.tensor_tensor(out=pairs[:], in0=sq[:, :, 0:2], in1=sq[:, :, 2:4], op=ADD)
-            return pairs
+        def pair_squares(u, h):
+            pairs = tile_of("pairs", u, [P, 2, 4 * UB, 2], F32)
+            sq = tiles["squares", u][:, 2 * h : 2 * h + 2, :].rearrange("p n (b i) -> p (n b) i", i=T)
+            nc.vector.tensor_tensor(out=pairs[:, h], in0=sq[:, :, 0:2], in1=sq[:, :, 2:4], op=ADD)
 
-        def filter_den(pairs):
-            den = work.tile([P, 8 * UB], F32, name="den")
+        def sum_squares(u, i):
+            den = tile_of("den", u, [P, 8 * UB], F32)
+            pairs = tiles["pairs", u][:].rearrange("p h n v -> p (h n) v")
             nc.vector.tensor_tensor(out=den[:], in0=pairs[:, :, 0], in1=pairs[:, :, 1], op=ADD)
-            root = work.tile([P, 8 * UB], F32, name="root")
-            nc.scalar.activation(out=root[:], in_=den[:], func=ACT.Abs_reciprocal_sqrt, bias=1.0)
-            inv = work.tile([P, 8 * UB], F32, name="inv")
-            nc.scalar.activation(out=inv[:], in_=root[:], func=ACT.Square)
-            return inv
 
-        def filter_num(sums, u):
-            num = work.tile([P, 8, UB], F32, name="num")
-            g_view = g_t[:].rearrange("p g e b -> p (g e b)").bitcast(BF16)
+        def invert(u, i):
+            root = tile_of("root", u, [P, 8 * UB], F32)
+            nc.scalar.activation(out=root[:], in_=tiles["den", u][:], func=ACT.Abs_reciprocal_sqrt, bias=1.0)
+            inv = tile_of("inv", u, [P, 8 * UB], F32)
+            nc.scalar.activation(out=inv[:], in_=root[:], func=ACT.Square)
+
+        def numerator(u, i):
+            num = tile_of("num", u, [P, 8, UB], F32)
+            g_view = g_t[:, u // 2].rearrange("p g e b -> p (g e b)").bitcast(BF16)
             g_view = g_view.rearrange("p (k b v) -> p k v b", k=4, v=2)
+            b0 = UB * (u % 2)
             nc.vector.tensor_tensor(
                 out=num[:].rearrange("p (k v) b -> p k v b", v=2),
-                in0=sums[:].rearrange("p (k v) b -> p k v b", v=2),
-                in1=g_view[:, :, :, UB * u : UB * (u + 1)],
+                in0=tiles["sums", u][:].rearrange("p (k v) b -> p k v b", v=2),
+                in1=g_view[:, :, :, b0 : b0 + UB],
                 op=MULT,
             )
-            return num
 
-        def filter_h(num, inv):
-            filt = work.tile([P, 8, UB], F32, name="filt")
+        def ridge(u, i):
+            filt = tile_of("filt", u, [P, 8, UB], F32)
             nc.vector.tensor_tensor(
                 out=filt[:].rearrange("p n b -> p (n b)"),
-                in0=num[:].rearrange("p n b -> p (n b)"),
-                in1=inv[:],
+                in0=tiles["num", u][:].rearrange("p n b -> p (n b)"),
+                in1=tiles["inv", u][:],
                 op=MULT,
             )
-            return filt
 
-        def x_stage(xq, filt):
-            codes, scales = xq
-            ys = []
-            for rt in range(RT):
-                y = work.tile([P, GROUPS, P, 4], BF16, name="y", bufs=3, align_bytes=64)
-                nb = P // T
-                for h in range(2):
-                    bank = psum.tile([P, 4, P], F32, name="bank_x", tag="mm", bufs=6)
-                    for t in range(4):
-                        for gr in range(GROUPS):
-                            nc.tensor.matmul_mx(
-                                out=bank[:, t, :],
-                                lhsT=phi_p[h][:, gr, t, :].bitcast(FP8X4),
-                                lhsT_scale=phi_sp[4 * gr : P, h, t, :],
-                                rhs=codes[:, gr, P * rt : P * (rt + 1)].bitcast(FP8X4),
-                                rhs_scale=scales[:, gr, P * rt : P * (rt + 1)],
-                                start=(gr == 0),
-                                stop=(gr == GROUPS - 1),
-                            )
-                    f = filt[:, 4 * h : 4 * h + 4, nb * rt : nb * (rt + 1)].rearrange("p t b -> p b t")
-                    nc.vector.tensor_tensor(
-                        out=y[:, h].rearrange("p (b j) t -> p b j t", j=T),
-                        in0=bank[:].rearrange("p t (b j) -> p b j t", j=T),
-                        in1=f.unsqueeze(2).to_broadcast([P, nb, T, 4]),
-                        op=MULT,
+        def x_bank(u, i):
+            rt, h = divmod(i, 2)
+            codes, scales, filt = tiles["codes_x", u], tiles["scales_x", u], tiles["filt", u]
+            y = tile_of("y%d" % rt, u, [P, GROUPS, P, 4], BF16)
+            bank = psum.tile([P, 4, P], F32, name="bank_x", tag="mm", bufs=5)
+            for t in range(4):
+                for gr in range(GROUPS):
+                    nc.tensor.matmul_mx(
+                        out=bank[:, t, :],
+                        lhsT=phi_p[h][:, gr, t, :].bitcast(FP8X4),
+                        lhsT_scale=phi_sp[h][4 * gr : P, t, :],
+                        rhs=codes[:, gr, P * rt : P * (rt + 1)].bitcast(FP8X4),
+                        rhs_scale=scales[:, gr, P * rt : P * (rt + 1)],
+                        start=(gr == 0),
+                        stop=(gr == GROUPS - 1),
                     )
-                ys.append(y)
-            return ys
+            nb = P // T
+            f = filt[:, 4 * h : 4 * h + 4, nb * rt : nb * (rt + 1)].rearrange("p t b -> p b t")
+            nc.vector.tensor_tensor(
+                out=y[:, h].rearrange("p (b j) t -> p b j t", j=T),
+                in0=bank[:].rearrange("p t (b j) -> p b j t", j=T),
+                in1=f.unsqueeze(2).to_broadcast([P, nb, T, 4]),
+                op=MULT,
+            )
 
-        def quantize_y(ys):
-            res = []
-            for y in ys:
-                codes = work.tile([P, GROUPS, P], U32, name="y_codes", bufs=3, align_bytes=64)
-                scales = work.tile([P, GROUPS, P], U8, name="y_scales", bufs=3, align_bytes=64)
-                nc.vector.quantize_mx(
-                    out=codes[:].rearrange("p g r -> p (g r)").bitcast(FP8X4),
-                    scales=scales[:].rearrange("p g r -> p (g r)"),
-                    in_=y[:].rearrange("p g r j -> p (g r j)"),
+        def quantize_y(u, rt):
+            quantize("y%d" % rt, u, tiles["y%d" % rt, u], [P, GROUPS, P])
+
+        def out_bank(u, i):
+            h, rt = divmod(i, 2)
+            codes, scales = tiles["codes_y%d" % rt, u], tiles["scales_y%d" % rt, u]
+            rows = tile_of("rows%d" % rt, u, [P, K], F32)
+            short = tile_of("short%d" % h, u, [P, RT, 512], BF16)
+            bank = psum.tile([P, 512], F32, name="bank_o", tag="mm", bufs=5)
+            cols = slice(512 * h, 512 * (h + 1))
+            for gr in range(GROUPS):
+                nc.tensor.matmul_mx(
+                    out=bank[:],
+                    lhsT=codes[:, gr, :].bitcast(FP8X4),
+                    lhsT_scale=scales[:, gr, :],
+                    rhs=psi_w[:, gr, cols].bitcast(FP8X4),
+                    rhs_scale=psi_s[4 * gr : P, cols],
+                    start=(gr == 0),
+                    stop=(gr == GROUPS - 1),
                 )
-                res.append((codes, scales))
-            return res
-
-        def out_stage(yq, u):
-            rounded = []
-            for rt in range(RT):
-                codes, scales = yq[rt]
-                rows = work.tile([P, K], F32, name="rows", bufs=3)
-                short = work.tile([P, K], BF16, name="short", bufs=4, align_bytes=64)
-                for h in range(2):
-                    bank = psum.tile([P, 512], F32, name="bank_o", tag="mm", bufs=6)
-                    cols = slice(512 * h, 512 * (h + 1))
-                    for gr in range(GROUPS):
-                        nc.tensor.matmul_mx(
-                            out=bank[:],
-                            lhsT=codes[:, gr, :].bitcast(FP8X4),
-                            lhsT_scale=scales[:, gr, :],
-                            rhs=psi_w[:, gr, cols].bitcast(FP8X4),
-                            rhs_scale=psi_s[4 * gr : P, cols],
-                            start=(gr == 0),
-                            stop=(gr == GROUPS - 1),
-                        )
-                    nc.scalar.copy(out=rows[:, cols], in_=bank[:])
-                    nc.gpsimd.tensor_scalar(
-                        out=short[:, cols].rearrange("p (e q v) -> p e q v", e=2, v=2),
-                        in0=rows[:, cols].rearrange("p (q e v) -> p e q v", e=2, v=2),
-                        scalar1=1.0,
-                        scalar2=0.0,
-                        op0=MULT,
-                        op1=ADD,
-                    )
+            nc.scalar.copy(out=rows[:, cols], in_=bank[:])
+            if h == 1:
                 r0 = UNIT * u + P * rt
                 nc.sync.dma_start(out=out_rows[r0 : r0 + P, :], in_=rows[:])
-                rounded.append(short)
-            return rounded
 
-        def plane_stage(rounded, u):
-            turned = work.tile([P, GROUPS, UNIT, 4], BF16, name="turned_o", tag="turned", bufs=3, align_bytes=64)
-            for gr in range(GROUPS):
-                bank = psum.tile([P, 2, UNIT], F32, name="bank_p", tag="tp", bufs=2)
-                for rt in range(RT):
-                    words = rounded[rt][:].bitcast(F32)
-                    for e in range(2):
-                        first = 256 * gr + 128 * e
-                        nc.tensor.transpose(bank[:, e, P * rt : P * (rt + 1)], words[:, first : first + P], ident[:])
-                nc.scalar.copy(
-                    out=turned[:, gr].rearrange("p r j -> p (r j)").bitcast(F32).rearrange("p (r e) -> p r e", e=2),
-                    in_=bank[:].rearrange("p e r -> p r e"),
-                )
-            codes = work.tile([P, GROUPS, UNIT], U32, name="o_codes", align_bytes=64)
-            scales = work.tile([P, GROUPS * UNIT], U8, name="o_scales", align_bytes=64)
+        def round_bank(u, i):
+            h, rt = divmod(i, 2)
+            short, rows = tiles["short%d" % h, u], tiles["rows%d" % rt, u]
+            nc.vector.tensor_copy(
+                out=short[:, rt, :].rearrange("p (e q v) -> p e q v", e=2, v=2),
+                in_=rows[:, 512 * h : 512 * (h + 1)].rearrange("p (q e v) -> p e q v", e=2, v=2),
+            )
+
+        def turn_out(u, gr):
+            turned = tile_of("turned_o%d" % gr, u, [P, UNIT, 4], BF16)
+            words = tiles["short%d" % gr, u][:].rearrange("p s k -> p (s k)").bitcast(F32)
+            bank = psum.tile([P, 2, UNIT], F32, name="bank_p", tag="tp", bufs=3)
+            for rt in range(RT):
+                for e in range(2):
+                    first = 256 * rt + P * e
+                    nc.tensor.transpose(bank[:, e, P * rt : P * (rt + 1)], words[:, first : first + P], ident[:])
+            bank_to_words(bank, turned[:])
+
+        def quantize_out(u, gr):
+            codes = tile_of("codes_o", u, [P, GROUPS, UNIT], U32)
+            scales = tile_of("scales_o", u, [P, GROUPS, UNIT], U8)
             nc.vector.quantize_mx(
-                out=codes[:].rearrange("p g r -> p (g r)").bitcast(FP8X4),
-                scales=scales[:],
-                in_=turned[:].rearrange("p g r j -> p (g r j)"),
+                out=codes[:, gr, :].bitcast(FP8X4),
+                scales=scales[:, gr, :],
+                in_=tiles["turned_o%d" % gr, u][:].rearrange("p r j -> p (r j)"),
             )
-            cols = slice(UNIT * u, UNIT * (u + 1))
-            nc.sync.dma_start(
-                out=out_1[:, :, cols, :].rearrange("g p m t -> p g (m t)").bitcast(I32), in_=codes[:].bitcast(I32)
-            )
-            for q in range(4):
+            if gr == GROUPS - 1:
+                cols = slice(UNIT * u, UNIT * (u + 1))
                 nc.sync.dma_start(
-                    out=out_2[:, 4 * q : 4 * q + 4, cols].bitcast(I32).rearrange("g r m -> r g m"),
-                    in_=scales[32 * q : 32 * q + 4, :].bitcast(I32).rearrange("r (g m) -> r g m", g=GROUPS),
+                    out=out_1[:, :, cols, :].rearrange("g p m t -> p g (m t)").bitcast(I32), in_=codes[:].bitcast(I32)
                 )
+                for q in range(4):
+                    nc.sync.dma_start(
+                        out=out_2[:, 4 * q : 4 * q + 4, cols].bitcast(I32).rearrange("g r m -> r g m"),
+                        in_=scales[32 * q : 32 * q + 4].rearrange("r g m -> r (g m)").bitcast(I32).rearrange("r (g m) -> r g m", g=GROUPS),
+                    )
 
-        zq, xq, zs, num, inv, filt, yq, short = {}, {}, {}, {}, {}, {}, {}, {}
-        zt = turn(z_in[0], "z")
-        permute_phi(0)
-        zq[0] = quantize(zt, "z")
-        nc.vector.tensor_copy(
-            out=phi_sp[:],
-            in_=phi_s[:].rearrange("p (h m t) -> p h t m", h=2, t=4),
-        )
-        permute_phi(1)
-        zs[0] = z_stage(zq[0], 0)
-        pairs = pair_sums(zs[0][0])
-        xt = turn(x_in[0], "x")
-        xq[0] = quantize(xt, "x")
-        zt = turn(z_in[1], "z")
-        inv[0] = filter_den(pairs)
-        zq[1] = quantize(zt, "z")
-        turn_g()
-        num[0] = filter_num(zs[0][1], 0)
-        filt[0] = filter_h(num[0], inv[0])
-
-        for k in range(UNITS):
-            if k + 1 < UNITS:
-                zs[k + 1] = z_stage(zq[k + 1], k + 1)
-                pairs = pair_sums(zs[k + 1][0])
-            if k >= 1:
-                short[k - 1] = out_stage(yq[k - 1], k - 1)
-            if k + 2 < UNITS:
-                zt = turn(z_in[k + 2], "z")
-            if k + 1 < UNITS:
-                inv[k + 1] = filter_den(pairs)
-            ys = x_stage(xq[k], filt[k])
-            if k + 2 < UNITS:
-                zq[k + 2] = quantize(zt, "z")
-            if k + 1 < UNITS:
-                num[k + 1] = filter_num(zs[k + 1][1], k + 1)
-            yq[k] = quantize_y(ys)
-            if k + 1 < UNITS:
-                xt = turn(x_in[k + 1], "x")
-                filt[k + 1] = filter_h(num[k + 1], inv[k + 1])
-                xq[k + 1] = quantize(xt, "x")
-            if k >= 1:
-                plane_stage(short[k - 1], k - 1)
-        short[UNITS - 1] = out_stage(yq[UNITS - 1], UNITS - 1)
-        plane_stage(short[UNITS - 1], UNITS - 1)
+        steps = {
+            "phi_words_of": phi_words_of,
+            "phi_scales_of": phi_scales_of,
+            "turn_z": turn_z,
+            "turn_x": turn_x,
+            "quantize_z": quantize_z,
+            "quantize_x": quantize_x,
+            "turn_g": turn_g,
+            "z_bank": z_bank,
+            "pair_squares": pair_squares,
+            "sum_squares": sum_squares,
+            "invert": invert,
+            "numerator": numerator,
+            "ridge": ridge,
+            "x_bank": x_bank,
+            "quantize_y": quantize_y,
+            "out_bank": out_bank,
+            "round_bank": round_bank,
+            "turn_out": turn_out,
+            "quantize_out": quantize_out,
+        }
+        last = max(behind for step, i, behind in SLOT)
+        for slot in range(UNITS + last):
+            for step, i, behind in SLOT:
+                if 0 <= slot - behind < UNITS:
+                    steps[step](slot - behind, i)

@@ -26,45 +26,42 @@ RT = UNIT // P
 
 SHORT_LIVED = ("squares", "pairs", "den", "root", "inv", "num", "turned_o0", "turned_o1")
 SLOT = (
-    ("z_bank", 3, 2),
-    ("pair_squares", 1, 2),
-    ("turn_out", 0, 5),
-    ("x_bank", 2, 3),
-    ("turn_x", 1, 2),
-    ("out_bank", 1, 4),
-    ("quantize_y", 0, 3),
-    ("turn_x", 0, 1),
-    ("out_bank", 2, 4),
-    ("phi_words_of", 1, 1),
-    ("quantize_x", 0, 2),
-    ("sum_squares", 0, 2),
-    ("quantize_out", 0, 5),
-    ("x_bank", 3, 3),
-    ("round_bank", 1, 4),
-    ("out_bank", 3, 4),
-    ("turn_out", 1, 5),
-    ("turn_g", 0, 2),
-    ("numerator", 0, 2),
-    ("z_bank", 0, 1),
     ("z_bank", 1, 1),
-    ("quantize_y", 1, 3),
-    ("pair_squares", 0, 1),
-    ("out_bank", 0, 3),
-    ("invert", 0, 2),
-    ("round_bank", 2, 4),
-    ("round_bank", 3, 4),
-    ("ridge", 0, 2),
-    ("quantize_out", 1, 5),
+    ("pair_squares", 0, 2),
     ("z_bank", 2, 1),
-    ("phi_scales_of", 0, 0),
+    ("round_bank", 0, 5),
+    ("sum_squares", 0, 2),
+    ("out_bank", 0, 4),
+    ("quantize_y", 1, 4),
+    ("round_bank", 2, 5),
     ("turn_z", 0, 0),
-    ("round_bank", 0, 3),
-    ("phi_words_of", 0, 0),
+    ("x_bank", 2, 3),
     ("turn_z", 1, 0),
+    ("quantize_out", 1, 6),
+    ("turn_g", 0, 0),
+    ("phi_scales_of", 1, 0),
+    ("x_bank", 3, 3),
+    ("quantize_x", 0, 1),
+    ("invert", 0, 2),
+    ("phi_words_of", 0, 0),
+    ("numerator", 0, 2),
+    ("quantize_z", 0, 0),
+    ("quantize_y", 0, 3),
+    ("ridge", 0, 2),
+    ("z_bank", 3, 1),
+    ("turn_out", 0, 5),
+    ("out_bank", 1, 4),
+    ("phi_scales_of", 0, 0),
+    ("phi_words_of", 1, 0),
+    ("quantize_out", 0, 5),
+    ("out_bank", 2, 4),
+    ("turn_x", 0, 0),
+    ("turn_x", 1, 0),
     ("x_bank", 0, 2),
     ("x_bank", 1, 2),
-    ("quantize_z", 0, 0),
-    ("phi_scales_of", 1, 0),
+    ("out_bank", 3, 4),
+    ("turn_out", 1, 5),
+    ("z_bank", 0, 0),
 )
 
 
@@ -126,16 +123,17 @@ def tile_learnedbasisridgecorrelationfilter_x2_kernel(
 
         load_rows("z", 0, split=2)
         load_scales(phi_s, phi_scales)
+        nc.sync.dma_start(out=g_in[:, 0, :], in_=g[0:P, :])
         load_phi(0)
         load_rows("x", 0)
         load_phi(1)
         load_rows("z", 1)
-        nc.sync.dma_start(out=g_in[:], in_=g.rearrange("(s p) k -> p s k", p=P))
         load_rows("x", 1)
         load_scales(psi_s, psi_scales)
         nc.sync.dma_start(out=psi_w[:], in_=psi_words.rearrange("g p n t -> p g (n t)").bitcast(I32))
         load_rows("z", 2)
         load_rows("x", 2)
+        nc.sync.dma_start(out=g_in[:, 1, :], in_=g[P : 2 * P, :])
         load_rows("z", 3)
         load_rows("x", 3)
 
@@ -231,13 +229,13 @@ def tile_learnedbasisridgecorrelationfilter_x2_kernel(
             )
 
         def pair_squares(u, h):
-            pairs = tile_of("pairs", u, [P, 2, 4 * UB, 2], F32)
-            sq = tiles["squares", u][:, 2 * h : 2 * h + 2, :].rearrange("p n (b i) -> p (n b) i", i=T)
-            nc.vector.tensor_tensor(out=pairs[:, h], in0=sq[:, :, 0:2], in1=sq[:, :, 2:4], op=ADD)
+            pairs = tile_of("pairs", u, [P, 8 * UB, 2], F32)
+            sq = tiles["squares", u][:].rearrange("p n (b i) -> p (n b) i", i=T)
+            nc.gpsimd.tensor_tensor(out=pairs[:], in0=sq[:, :, 0:2], in1=sq[:, :, 2:4], op=ADD)
 
         def sum_squares(u, i):
             den = tile_of("den", u, [P, 8 * UB], F32)
-            pairs = tiles["pairs", u][:].rearrange("p h n v -> p (h n) v")
+            pairs = tiles["pairs", u]
             nc.vector.tensor_tensor(out=den[:], in0=pairs[:, :, 0], in1=pairs[:, :, 1], op=ADD)
 
         def invert(u, i):
@@ -251,7 +249,7 @@ def tile_learnedbasisridgecorrelationfilter_x2_kernel(
             g_view = g_t[:, u // 2].rearrange("p g e b -> p (g e b)").bitcast(BF16)
             g_view = g_view.rearrange("p (k b v) -> p k v b", k=4, v=2)
             b0 = UB * (u % 2)
-            nc.vector.tensor_tensor(
+            nc.gpsimd.tensor_tensor(
                 out=num[:].rearrange("p (k v) b -> p k v b", v=2),
                 in0=tiles["sums", u][:].rearrange("p (k v) b -> p k v b", v=2),
                 in1=g_view[:, :, :, b0 : b0 + UB],
@@ -298,8 +296,7 @@ def tile_learnedbasisridgecorrelationfilter_x2_kernel(
         def out_bank(u, i):
             h, rt = divmod(i, 2)
             codes, scales = tiles["codes_y%d" % rt, u], tiles["scales_y%d" % rt, u]
-            rows = tile_of("rows%d" % rt, u, [P, K], F32)
-            short = tile_of("short%d" % h, u, [P, RT, 512], BF16)
+            rows = tile_of("rows", u, [P, RT, K], F32)
             bank = psum.tile([P, 512], F32, name="bank_o", tag="mm", bufs=5)
             cols = slice(512 * h, 512 * (h + 1))
             for gr in range(GROUPS):
@@ -312,22 +309,23 @@ def tile_learnedbasisridgecorrelationfilter_x2_kernel(
                     start=(gr == 0),
                     stop=(gr == GROUPS - 1),
                 )
-            nc.scalar.copy(out=rows[:, cols], in_=bank[:])
+            nc.scalar.copy(out=rows[:, rt, cols], in_=bank[:])
             if h == 1:
                 r0 = UNIT * u + P * rt
-                nc.sync.dma_start(out=out_rows[r0 : r0 + P, :], in_=rows[:])
+                nc.sync.dma_start(out=out_rows[r0 : r0 + P, :], in_=rows[:, rt, :])
 
         def round_bank(u, i):
-            h, rt = divmod(i, 2)
-            short, rows = tiles["short%d" % h, u], tiles["rows%d" % rt, u]
+            h = i // 2
+            short = tile_of("short%d" % h, u, [P, RT, 2, P, 2], BF16)
+            rows = tiles["rows", u]
             nc.vector.tensor_copy(
-                out=short[:, rt, :].rearrange("p (e q v) -> p e q v", e=2, v=2),
-                in_=rows[:, 512 * h : 512 * (h + 1)].rearrange("p (q e v) -> p e q v", e=2, v=2),
+                out=short[:],
+                in_=rows[:, :, 512 * h : 512 * (h + 1)].rearrange("p s (q e v) -> p s e q v", e=2, v=2),
             )
 
         def turn_out(u, gr):
             turned = tile_of("turned_o%d" % gr, u, [P, UNIT, 4], BF16)
-            words = tiles["short%d" % gr, u][:].rearrange("p s k -> p (s k)").bitcast(F32)
+            words = tiles["short%d" % gr, u][:].rearrange("p s e q v -> p (s e q v)").bitcast(F32)
             bank = psum.tile([P, 2, UNIT], F32, name="bank_p", tag="tp", bufs=3)
             for rt in range(RT):
                 for e in range(2):

@@ -26,42 +26,45 @@ RT = UNIT // P
 
 SHORT_LIVED = ("squares", "pairs", "den", "root", "inv", "num", "turned_o0", "turned_o1")
 SLOT = (
-    ("z_bank", 1, 1),
+    ("turn_z", 1, 1),
+    ("warm_up", 2, 1),
+    ("out_bank", 0, 5),
+    ("phi_scales_of", 0, 1),
+    ("x_bank", 2, 4),
+    ("quantize_y", 0, 4),
     ("pair_squares", 0, 2),
-    ("z_bank", 2, 1),
+    ("quantize_z", 0, 1),
+    ("invert", 0, 3),
+    ("x_bank", 3, 4),
+    ("z_bank", 2, 2),
+    ("phi_words_of", 0, 1),
+    ("z_bank", 3, 2),
+    ("numerator", 0, 3),
+    ("turn_x", 0, 1),
+    ("turn_x", 1, 1),
+    ("warm_up", 3, 1),
+    ("turn_out", 0, 6),
+    ("pair_squares", 1, 2),
+    ("out_bank", 1, 5),
+    ("ridge", 0, 3),
+    ("out_bank", 2, 5),
     ("round_bank", 0, 5),
-    ("sum_squares", 0, 2),
-    ("out_bank", 0, 4),
     ("quantize_y", 1, 4),
-    ("round_bank", 2, 5),
-    ("turn_z", 0, 0),
-    ("x_bank", 2, 3),
-    ("turn_z", 1, 0),
-    ("quantize_out", 1, 6),
-    ("turn_g", 0, 0),
-    ("phi_scales_of", 1, 0),
-    ("x_bank", 3, 3),
+    ("out_bank", 3, 5),
+    ("turn_out", 1, 6),
+    ("quantize_out", 0, 6),
+    ("phi_scales_of", 1, 1),
+    ("turn_g", 0, 2),
     ("quantize_x", 0, 1),
-    ("invert", 0, 2),
-    ("phi_words_of", 0, 0),
-    ("numerator", 0, 2),
-    ("quantize_z", 0, 0),
-    ("quantize_y", 0, 3),
-    ("ridge", 0, 2),
-    ("z_bank", 3, 1),
-    ("turn_out", 0, 5),
-    ("out_bank", 1, 4),
-    ("phi_scales_of", 0, 0),
-    ("phi_words_of", 1, 0),
-    ("quantize_out", 0, 5),
-    ("out_bank", 2, 4),
-    ("turn_x", 0, 0),
-    ("turn_x", 1, 0),
-    ("x_bank", 0, 2),
-    ("x_bank", 1, 2),
-    ("out_bank", 3, 4),
-    ("turn_out", 1, 5),
-    ("z_bank", 0, 0),
+    ("sum_squares", 0, 2),
+    ("phi_words_of", 1, 1),
+    ("x_bank", 0, 3),
+    ("x_bank", 1, 3),
+    ("z_bank", 0, 1),
+    ("round_bank", 2, 5),
+    ("quantize_out", 1, 6),
+    ("z_bank", 1, 1),
+    ("turn_z", 0, 0),
 )
 
 
@@ -89,6 +92,17 @@ def tile_learnedbasisridgecorrelationfilter_x2_kernel(
         psi_s = keep.tile([P, K], U8, name="psi_s", align_bytes=64)
         nc.vector.memset(phi_s[:].bitcast(I32), 0)
         nc.vector.memset(psi_s[:].bitcast(I32), 0)
+
+        blank = keep.tile([P, 512], BF16, name="blank")
+        nc.vector.memset(blank[:], 0.0)
+
+        def warm_up(u, n):
+            if u == 0:
+                bank = psum.tile([P, 512], F32, name="bank_w", tag="mm", bufs=5)
+                for i in range(n):
+                    nc.tensor.matmul(bank[:], lhsT=blank[:, 0:P], rhs=blank[:], start=True, stop=True)
+
+        warm_up(0, 5)
 
         phi_raw = [keep.tile([P, GROUPS, 512], I32, name="phi_raw%d" % h, align_bytes=64) for h in range(2)]
         phi_p = [keep.tile([P, GROUPS, 4, P], I32, name="phi_p%d" % h, align_bytes=64) for h in range(2)]
@@ -123,11 +137,11 @@ def tile_learnedbasisridgecorrelationfilter_x2_kernel(
 
         load_rows("z", 0, split=2)
         load_scales(phi_s, phi_scales)
-        nc.sync.dma_start(out=g_in[:, 0, :], in_=g[0:P, :])
-        load_phi(0)
         load_rows("x", 0)
+        load_phi(0)
         load_phi(1)
         load_rows("z", 1)
+        nc.sync.dma_start(out=g_in[:, 0, :], in_=g[0:P, :])
         load_rows("x", 1)
         load_scales(psi_s, psi_scales)
         nc.sync.dma_start(out=psi_w[:], in_=psi_words.rearrange("g p n t -> p g (n t)").bitcast(I32))
@@ -155,11 +169,15 @@ def tile_learnedbasisridgecorrelationfilter_x2_kernel(
                     out=phi_sp[h][:], in_=phi_s[:, 512 * h : 512 * (h + 1)].rearrange("p (m t) -> p t m", t=4)
                 )
 
-        def bank_to_words(bank, dst):
-            nc.scalar.copy(
-                out=dst.rearrange("p r j -> p (r j)").bitcast(F32).rearrange("p (r e) -> p r e", e=2),
-                in_=bank[:].rearrange("p e r -> p r e"),
-            )
+        def bank_to_words(bank, dst, by_template=False):
+            words = dst.rearrange("p r j -> p (r j)").bitcast(F32)
+            if by_template:
+                nc.scalar.copy(
+                    out=words.rearrange("p (i b e) -> p i b e", i=T, e=2),
+                    in_=bank[:].rearrange("p e (b i) -> p i b e", i=T),
+                )
+            else:
+                nc.scalar.copy(out=words.rearrange("p (r e) -> p r e", e=2), in_=bank[:].rearrange("p e r -> p r e"))
 
         def turn(src, u, gr):
             turned = tile_of("turned_" + src, u, [P, GROUPS, UNIT, 4], BF16)
@@ -169,7 +187,7 @@ def tile_learnedbasisridgecorrelationfilter_x2_kernel(
                 for e in range(2):
                     first = 512 * s + 256 * gr
                     nc.tensor.transpose(bank[:, e, P * s : P * (s + 1)], words[:, first + e : first + 256 : 2], ident[:])
-            bank_to_words(bank, turned[:, gr])
+            bank_to_words(bank, turned[:, gr], by_template=(src == "z"))
 
         def turn_z(u, gr):
             turn("z", u, gr)
@@ -223,24 +241,25 @@ def tile_learnedbasisridgecorrelationfilter_x2_kernel(
             nc.scalar.activation(out=squares[:, n, :], in_=bank[:].rearrange("p t r -> p (t r)"), func=ACT.Square)
             nc.vector.tensor_reduce(
                 out=sums[:, 2 * n : 2 * n + 2, :],
-                in_=bank[:].rearrange("p t (b i) -> p t b i", i=T),
+                in_=bank[:].rearrange("p t (i b) -> p t b i", i=T),
                 axis=AXIS_X,
                 op=ADD,
             )
 
         def pair_squares(u, h):
-            pairs = tile_of("pairs", u, [P, 8 * UB, 2], F32)
-            sq = tiles["squares", u][:].rearrange("p n (b i) -> p (n b) i", i=T)
-            nc.gpsimd.tensor_tensor(out=pairs[:], in0=sq[:, :, 0:2], in1=sq[:, :, 2:4], op=ADD)
+            pairs = tile_of("pairs", u, [P, 8, 2 * UB], F32)
+            sq = tiles["squares", u][:].rearrange("p n (t r) -> p (n t) r", t=2)
+            n = slice(4 * h, 4 * h + 4)
+            nc.vector.tensor_tensor(out=pairs[:, n], in0=sq[:, n, 0 : 2 * UB], in1=sq[:, n, 2 * UB : 4 * UB], op=ADD)
 
         def sum_squares(u, i):
-            den = tile_of("den", u, [P, 8 * UB], F32)
+            den = tile_of("den", u, [P, 8, UB], F32)
             pairs = tiles["pairs", u]
-            nc.vector.tensor_tensor(out=den[:], in0=pairs[:, :, 0], in1=pairs[:, :, 1], op=ADD)
+            nc.gpsimd.tensor_tensor(out=den[:], in0=pairs[:, :, 0:UB], in1=pairs[:, :, UB : 2 * UB], op=ADD)
 
         def invert(u, i):
             root = tile_of("root", u, [P, 8 * UB], F32)
-            nc.scalar.activation(out=root[:], in_=tiles["den", u][:], func=ACT.Abs_reciprocal_sqrt, bias=1.0)
+            nc.scalar.activation(out=root[:], in_=tiles["den", u][:].rearrange("p n b -> p (n b)"), func=ACT.Abs_reciprocal_sqrt, bias=1.0)
             inv = tile_of("inv", u, [P, 8 * UB], F32)
             nc.scalar.activation(out=inv[:], in_=root[:], func=ACT.Square)
 
@@ -258,7 +277,7 @@ def tile_learnedbasisridgecorrelationfilter_x2_kernel(
 
         def ridge(u, i):
             filt = tile_of("filt", u, [P, 8, UB], F32)
-            nc.vector.tensor_tensor(
+            nc.gpsimd.tensor_tensor(
                 out=filt[:].rearrange("p n b -> p (n b)"),
                 in0=tiles["num", u][:].rearrange("p n b -> p (n b)"),
                 in1=tiles["inv", u][:],
@@ -355,6 +374,7 @@ def tile_learnedbasisridgecorrelationfilter_x2_kernel(
         steps = {
             "phi_words_of": phi_words_of,
             "phi_scales_of": phi_scales_of,
+            "warm_up": warm_up,
             "turn_z": turn_z,
             "turn_x": turn_x,
             "quantize_z": quantize_z,

@@ -84,14 +84,22 @@ def tile_learnedbasisridgecorrelationfilter_x2_kernel(
         make_identity(nc, ident[:])
         ctx.enter_context(tc.manual_schedule())
 
+        phi_s = keep.tile([P, K], U8, name="phi_s", align_bytes=64)
+        psi_s = keep.tile([P, K], U8, name="psi_s", align_bytes=64)
+        nc.vector.memset(phi_s[:].bitcast(I32), 0)
+
+        def load_scales(queue, plane, scales):
+            for q in range(4):
+                queue.dma_start(
+                    out=plane[32 * q : 32 * q + 8, :].bitcast(I32),
+                    in_=scales[:, 4 * q : 4 * q + 4, :].bitcast(I32),
+                )
+
+        load_scales(nc.scalar, phi_s, phi_scales)
         warm = keep.tile([P, 1], F32, name="warm")
         nc.vector.memset(warm[:], 1.0)
         warm_out = keep.tile([P, 1], F32, name="warm_out")
         nc.scalar.activation(out=warm_out[:], in_=warm[:], func=ACT.Abs_reciprocal_sqrt)
-        phi_s = keep.tile([P, K], U8, name="phi_s", align_bytes=64)
-        psi_s = keep.tile([P, K], U8, name="psi_s", align_bytes=64)
-        nc.vector.memset(phi_s[:].bitcast(I32), 0)
-        nc.vector.memset(psi_s[:].bitcast(I32), 0)
 
         blank = keep.tile([P, 512], BF16, name="blank")
         nc.vector.memset(blank[:], 0.0)
@@ -103,6 +111,7 @@ def tile_learnedbasisridgecorrelationfilter_x2_kernel(
                     nc.tensor.matmul(bank[:], lhsT=blank[:, 0:P], rhs=blank[:], start=True, stop=True)
 
         warm_up(0, 5)
+        nc.vector.memset(psi_s[:].bitcast(I32), 0)
 
         phi_raw = [keep.tile([P, GROUPS, 512], I32, name="phi_raw%d" % h, align_bytes=64) for h in range(2)]
         phi_p = [keep.tile([P, GROUPS, 4, P], I32, name="phi_p%d" % h, align_bytes=64) for h in range(2)]
@@ -112,22 +121,15 @@ def tile_learnedbasisridgecorrelationfilter_x2_kernel(
         g_t = keep.tile([P, 2, GROUPS, 2, P], F32, name="g_t", align_bytes=64)
         t_in = {}
 
-        def load_rows(src, u, split=1):
+        def load_rows(src, u, parts=1):
             t = keep.tile([P, RT, K], BF16, name="%s%d" % (src, u), align_bytes=64)
-            for s in range(split):
-                n = RT // split
+            width = K // parts
+            for c in range(0, K, width):
                 nc.sync.dma_start(
-                    out=t[:, n * s : n * (s + 1), :],
-                    in_=in_rows[src][UNIT * u + P * n * s : UNIT * u + P * n * (s + 1), :].rearrange("(s p) k -> p s k", p=P),
+                    out=t[:, :, c : c + width],
+                    in_=in_rows[src][UNIT * u : UNIT * (u + 1), c : c + width].rearrange("(s p) k -> p s k", p=P),
                 )
             t_in[src, u] = t
-
-        def load_scales(plane, scales):
-            for q in range(4):
-                nc.sync.dma_start(
-                    out=plane[32 * q : 32 * q + 8, :].bitcast(I32),
-                    in_=scales[:, 4 * q : 4 * q + 4, :].bitcast(I32),
-                )
 
         def load_phi(h):
             nc.sync.dma_start(
@@ -135,21 +137,20 @@ def tile_learnedbasisridgecorrelationfilter_x2_kernel(
                 in_=phi_words[:, :, 512 * h : 512 * (h + 1), :].rearrange("g p n t -> p g (n t)").bitcast(I32),
             )
 
-        load_rows("z", 0, split=2)
-        load_scales(phi_s, phi_scales)
-        load_rows("x", 0)
+        load_rows("z", 0, parts=2)
+        load_rows("x", 0, parts=2)
         load_phi(0)
         load_phi(1)
         load_rows("z", 1)
         nc.sync.dma_start(out=g_in[:, 0, :], in_=g[0:P, :])
         load_rows("x", 1)
-        load_scales(psi_s, psi_scales)
-        nc.sync.dma_start(out=psi_w[:], in_=psi_words.rearrange("g p n t -> p g (n t)").bitcast(I32))
         load_rows("z", 2)
         load_rows("x", 2)
         nc.sync.dma_start(out=g_in[:, 1, :], in_=g[P : 2 * P, :])
         load_rows("z", 3)
         load_rows("x", 3)
+        nc.sync.dma_start(out=psi_w[:], in_=psi_words.rearrange("g p n t -> p g (n t)").bitcast(I32))
+        load_scales(nc.sync, psi_s, psi_scales)
 
         tiles = {}
 

from contextlib import ExitStack

import concourse.mybir as mybir
from concourse.masks import make_identity

F32 = mybir.dt.float32
BF16 = mybir.dt.bfloat16
I32 = mybir.dt.int32
U32 = mybir.dt.uint32
U8 = mybir.dt.uint8
FP8X4 = mybir.dt.float8_e4m3fn_x4
ADD = mybir.AluOpType.add
MULT = mybir.AluOpType.mult
ACT = mybir.ActivationFunctionType
AXIS_X = mybir.AxisListType.X

B, T, K = 256, 4, 1024
ROWS = B * T
FLOPS = 3 * 2 * ROWS * K * K
P = 128
GROUPS = K // 512
UNIT = 256
UB = UNIT // T
UNITS = ROWS // UNIT
RT = UNIT // P

SHORT_LIVED = ("squares", "pairs", "den", "root", "inv", "num", "turned_o0", "turned_o1")
SLOT = (
    ("turn_z", 1, 1),
    ("warm_up", 2, 1),
    ("out_bank", 0, 5),
    ("phi_scales_of", 0, 1),
    ("x_bank", 2, 4),
    ("quantize_y", 0, 4),
    ("pair_squares", 0, 2),
    ("quantize_z", 0, 1),
    ("invert", 0, 3),
    ("x_bank", 3, 4),
    ("z_bank", 2, 2),
    ("phi_words_of", 0, 1),
    ("z_bank", 3, 2),
    ("numerator", 0, 3),
    ("turn_x", 0, 1),
    ("turn_x", 1, 1),
    ("warm_up", 3, 1),
    ("turn_out", 0, 6),
    ("pair_squares", 1, 2),
    ("out_bank", 1, 5),
    ("ridge", 0, 3),
    ("out_bank", 2, 5),
    ("round_bank", 0, 5),
    ("quantize_y", 1, 4),
    ("out_bank", 3, 5),
    ("turn_out", 1, 6),
    ("quantize_out", 0, 6),
    ("phi_scales_of", 1, 1),
    ("turn_g", 0, 2),
    ("quantize_x", 0, 1),
    ("sum_squares", 0, 2),
    ("phi_words_of", 1, 1),
    ("x_bank", 0, 3),
    ("x_bank", 1, 3),
    ("z_bank", 0, 1),
    ("round_bank", 2, 5),
    ("quantize_out", 1, 6),
    ("z_bank", 1, 1),
    ("turn_z", 0, 0),
)


def tile_learnedbasisridgecorrelationfilter_x2_kernel(
    tc, z, x, phi_words, phi_scales, g, psi_words, psi_scales, out_0, out_1, out_2
):
    nc = tc.nc
    out_rows = out_0.flatten_outer_dims()
    in_rows = {"z": z.flatten_outer_dims(), "x": x.flatten_outer_dims()}

    with ExitStack() as ctx:
        keep = ctx.enter_context(tc.tile_pool(name="keep", bufs=1))
        work = ctx.enter_context(tc.tile_pool(name="work", bufs=3))
        psum = ctx.enter_context(tc.psum_pool(name="psum", bufs=1))

        ident = keep.tile([P, P], F32, name="ident")
        make_identity(nc, ident[:])
        ctx.enter_context(tc.manual_schedule())

        phi_s = keep.tile([P, K], U8, name="phi_s", align_bytes=64)
        psi_s = keep.tile([P, K], U8, name="psi_s", align_bytes=64)
        nc.vector.memset(phi_s[:].bitcast(I32), 0)

        def load_scales(queue, plane, scales):
            for q in range(4):
                queue.dma_start(
                    out=plane[32 * q : 32 * q + 8, :].bitcast(I32),
                    in_=scales[:, 4 * q : 4 * q + 4, :].bitcast(I32),
                )

        load_scales(nc.scalar, phi_s, phi_scales)
        warm = keep.tile([P, 1], F32, name="warm")
        nc.vector.memset(warm[:], 1.0)
        warm_out = keep.tile([P, 1], F32, name="warm_out")
        nc.scalar.activation(out=warm_out[:], in_=warm[:], func=ACT.Abs_reciprocal_sqrt)

        blank = keep.tile([P, 512], BF16, name="blank")
        nc.vector.memset(blank[:], 0.0)

        def warm_up(u, n):
            if u == 0:
                bank = psum.tile([P, 512], F32, name="bank_w", tag="mm", bufs=5)
                for i in range(n):
                    nc.tensor.matmul(bank[:], lhsT=blank[:, 0:P], rhs=blank[:], start=True, stop=True)

        warm_up(0, 5)
        nc.vector.memset(psi_s[:].bitcast(I32), 0)

        phi_raw = [keep.tile([P, GROUPS, 512], I32, name="phi_raw%d" % h, align_bytes=64) for h in range(2)]
        phi_p = [keep.tile([P, GROUPS, 4, P], I32, name="phi_p%d" % h, align_bytes=64) for h in range(2)]
        phi_sp = [keep.tile([P, 4, P], U8, name="phi_sp%d" % h, align_bytes=64) for h in range(2)]
        psi_w = keep.tile([P, GROUPS, K], I32, name="psi_w", align_bytes=64)
        g_in = keep.tile([P, 2, K], BF16, name="g_in", align_bytes=64)
        g_t = keep.tile([P, 2, GROUPS, 2, P], F32, name="g_t", align_bytes=64)
        t_in = {}

        def load_rows(src, u, parts=1):
            t = keep.tile([P, RT, K], BF16, name="%s%d" % (src, u), align_bytes=64)
            width = K // parts
            for c in range(0, K, width):
                nc.sync.dma_start(
                    out=t[:, :, c : c + width],
                    in_=in_rows[src][UNIT * u : UNIT * (u + 1), c : c + width].rearrange("(s p) k -> p s k", p=P),
                )
            t_in[src, u] = t

        def load_phi(h):
            nc.sync.dma_start(
                out=phi_raw[h][:],
                in_=phi_words[:, :, 512 * h : 512 * (h + 1), :].rearrange("g p n t -> p g (n t)").bitcast(I32),
            )

        load_rows("z", 0, parts=2)
        load_rows("x", 0, parts=2)
        load_phi(0)
        load_phi(1)
        load_rows("z", 1)
        nc.sync.dma_start(out=g_in[:, 0, :], in_=g[0:P, :])
        load_rows("x", 1)
        load_rows("z", 2)
        load_rows("x", 2)
        nc.sync.dma_start(out=g_in[:, 1, :], in_=g[P : 2 * P, :])
        load_rows("z", 3)
        load_rows("x", 3)
        nc.sync.dma_start(out=psi_w[:], in_=psi_words.rearrange("g p n t -> p g (n t)").bitcast(I32))
        load_scales(nc.sync, psi_s, psi_scales)

        tiles = {}

        def tile_of(key, u, shape, dtype):
            if (key, u) not in tiles:
                bufs = 2 if key in SHORT_LIVED else 3
                tiles[key, u] = work.tile(shape, dtype, name=key, tag=key, bufs=bufs, align_bytes=64)
            return tiles[key, u]

        def phi_words_of(u, h):
            if u == 0:
                nc.vector.tensor_copy(out=phi_p[h][:], in_=phi_raw[h][:].rearrange("p g (m t) -> p g t m", t=4))

        def phi_scales_of(u, h):
            if u == 0:
                nc.vector.tensor_copy(
                    out=phi_sp[h][:], in_=phi_s[:, 512 * h : 512 * (h + 1)].rearrange("p (m t) -> p t m", t=4)
                )

        def bank_to_words(bank, dst, by_template=False):
            words = dst.rearrange("p r j -> p (r j)").bitcast(F32)
            if by_template:
                nc.scalar.copy(
                    out=words.rearrange("p (i b e) -> p i b e", i=T, e=2),
                    in_=bank[:].rearrange("p e (b i) -> p i b e", i=T),
                )
            else:
                nc.scalar.copy(out=words.rearrange("p (r e) -> p r e", e=2), in_=bank[:].rearrange("p e r -> p r e"))

        def turn(src, u, gr):
            turned = tile_of("turned_" + src, u, [P, GROUPS, UNIT, 4], BF16)
            words = t_in[src, u][:].rearrange("p s k -> p (s k)").bitcast(F32)
            bank = psum.tile([P, 2, UNIT], F32, name="bank_t", tag="tp", bufs=3)
            for s in range(RT):
                for e in range(2):
                    first = 512 * s + 256 * gr
                    nc.tensor.transpose(bank[:, e, P * s : P * (s + 1)], words[:, first + e : first + 256 : 2], ident[:])
            bank_to_words(bank, turned[:, gr], by_template=(src == "z"))

        def turn_z(u, gr):
            turn("z", u, gr)

        def turn_x(u, gr):
            turn("x", u, gr)

        def quantize(key, u, turned, shape):
            codes = tile_of("codes_" + key, u, shape, U32)
            scales = tile_of("scales_" + key, u, shape, U8)
            nc.vector.quantize_mx(
                out=codes[:].rearrange("p g r -> p (g r)").bitcast(FP8X4),
                scales=scales[:].rearrange("p g r -> p (g r)"),
                in_=turned[:].rearrange("p g r j -> p (g r j)"),
            )

        def quantize_z(u, i):
            quantize("z", u, tiles["turned_z", u], [P, GROUPS, UNIT])

        def quantize_x(u, i):
            quantize("x", u, tiles["turned_x", u], [P, GROUPS, UNIT])

        def turn_g(u, i):
            if u % 2 == 0:
                s = u // 2
                words = g_in[:, s, :].bitcast(F32)
                bank = psum.tile([P, GROUPS, 2, P], F32, name="bank_g", tag="tp", bufs=3)
                for gr in range(GROUPS):
                    for e in range(2):
                        nc.tensor.transpose(bank[:, gr, e, :], words[:, 256 * gr + e : 256 * (gr + 1) : 2], ident[:])
                nc.scalar.copy(out=g_t[:, s], in_=bank[:])

        def z_bank(u, n):
            codes, scales = tiles["codes_z", u], tiles["scales_z", u]
            squares = tile_of("squares", u, [P, 4, 512], F32)
            sums = tile_of("sums", u, [P, 8, UB], F32)
            h = n // 2
            bank = psum.tile([P, 2, UNIT], F32, name="bank_z", tag="mm", bufs=5)
            for ti in range(2):
                t = 2 * (n % 2) + ti
                for gr in range(GROUPS):
                    nc.tensor.matmul_mx(
                        out=bank[:, ti, :],
                        lhsT=phi_p[h][:, gr, t, :].bitcast(FP8X4),
                        lhsT_scale=phi_sp[h][4 * gr : P, t, :],
                        rhs=codes[:, gr, :].bitcast(FP8X4),
                        rhs_scale=scales[:, gr, :],
                        start=(gr == 0),
                        stop=(gr == GROUPS - 1),
                    )
            nc.scalar.activation(out=squares[:, n, :], in_=bank[:].rearrange("p t r -> p (t r)"), func=ACT.Square)
            nc.vector.tensor_reduce(
                out=sums[:, 2 * n : 2 * n + 2, :],
                in_=bank[:].rearrange("p t (i b) -> p t b i", i=T),
                axis=AXIS_X,
                op=ADD,
            )

        def pair_squares(u, h):
            pairs = tile_of("pairs", u, [P, 8, 2 * UB], F32)
            sq = tiles["squares", u][:].rearrange("p n (t r) -> p (n t) r", t=2)
            n = slice(4 * h, 4 * h + 4)
            nc.vector.tensor_tensor(out=pairs[:, n], in0=sq[:, n, 0 : 2 * UB], in1=sq[:, n, 2 * UB : 4 * UB], op=ADD)

        def sum_squares(u, i):
            den = tile_of("den", u, [P, 8, UB], F32)
            pairs = tiles["pairs", u]
            nc.gpsimd.tensor_tensor(out=den[:], in0=pairs[:, :, 0:UB], in1=pairs[:, :, UB : 2 * UB], op=ADD)

        def invert(u, i):
            root = tile_of("root", u, [P, 8 * UB], F32)
            nc.scalar.activation(out=root[:], in_=tiles["den", u][:].rearrange("p n b -> p (n b)"), func=ACT.Abs_reciprocal_sqrt, bias=1.0)
            inv = tile_of("inv", u, [P, 8 * UB], F32)
            nc.scalar.activation(out=inv[:], in_=root[:], func=ACT.Square)

        def numerator(u, i):
            num = tile_of("num", u, [P, 8, UB], F32)
            g_view = g_t[:, u // 2].rearrange("p g e b -> p (g e b)").bitcast(BF16)
            g_view = g_view.rearrange("p (k b v) -> p k v b", k=4, v=2)
            b0 = UB * (u % 2)
            nc.gpsimd.tensor_tensor(
                out=num[:].rearrange("p (k v) b -> p k v b", v=2),
                in0=tiles["sums", u][:].rearrange("p (k v) b -> p k v b", v=2),
                in1=g_view[:, :, :, b0 : b0 + UB],
                op=MULT,
            )

        def ridge(u, i):
            filt = tile_of("filt", u, [P, 8, UB], F32)
            nc.gpsimd.tensor_tensor(
                out=filt[:].rearrange("p n b -> p (n b)"),
                in0=tiles["num", u][:].rearrange("p n b -> p (n b)"),
                in1=tiles["inv", u][:],
                op=MULT,
            )

        def x_bank(u, i):
            rt, h = divmod(i, 2)
            codes, scales, filt = tiles["codes_x", u], tiles["scales_x", u], tiles["filt", u]
            y = tile_of("y%d" % rt, u, [P, GROUPS, P, 4], BF16)
            bank = psum.tile([P, 4, P], F32, name="bank_x", tag="mm", bufs=5)
            for t in range(4):
                for gr in range(GROUPS):
                    nc.tensor.matmul_mx(
                        out=bank[:, t, :],
                        lhsT=phi_p[h][:, gr, t, :].bitcast(FP8X4),
                        lhsT_scale=phi_sp[h][4 * gr : P, t, :],
                        rhs=codes[:, gr, P * rt : P * (rt + 1)].bitcast(FP8X4),
                        rhs_scale=scales[:, gr, P * rt : P * (rt + 1)],
                        start=(gr == 0),
                        stop=(gr == GROUPS - 1),
                    )
            nb = P // T
            f = filt[:, 4 * h : 4 * h + 4, nb * rt : nb * (rt + 1)].rearrange("p t b -> p b t")
            nc.vector.tensor_tensor(
                out=y[:, h].rearrange("p (b j) t -> p b j t", j=T),
                in0=bank[:].rearrange("p t (b j) -> p b j t", j=T),
                in1=f.unsqueeze(2).to_broadcast([P, nb, T, 4]),
                op=MULT,
            )

        def quantize_y(u, rt):
            quantize("y%d" % rt, u, tiles["y%d" % rt, u], [P, GROUPS, P])

        def out_bank(u, i):
            h, rt = divmod(i, 2)
            codes, scales = tiles["codes_y%d" % rt, u], tiles["scales_y%d" % rt, u]
            rows = tile_of("rows", u, [P, RT, K], F32)
            bank = psum.tile([P, 512], F32, name="bank_o", tag="mm", bufs=5)
            cols = slice(512 * h, 512 * (h + 1))
            for gr in range(GROUPS):
                nc.tensor.matmul_mx(
                    out=bank[:],
                    lhsT=codes[:, gr, :].bitcast(FP8X4),
                    lhsT_scale=scales[:, gr, :],
                    rhs=psi_w[:, gr, cols].bitcast(FP8X4),
                    rhs_scale=psi_s[4 * gr : P, cols],
                    start=(gr == 0),
                    stop=(gr == GROUPS - 1),
                )
            nc.scalar.copy(out=rows[:, rt, cols], in_=bank[:])
            if h == 1:
                r0 = UNIT * u + P * rt
                nc.sync.dma_start(out=out_rows[r0 : r0 + P, :], in_=rows[:, rt, :])

        def round_bank(u, i):
            h = i // 2
            short = tile_of("short%d" % h, u, [P, RT, 2, P, 2], BF16)
            rows = tiles["rows", u]
            nc.vector.tensor_copy(
                out=short[:],
                in_=rows[:, :, 512 * h : 512 * (h + 1)].rearrange("p s (q e v) -> p s e q v", e=2, v=2),
            )

        def turn_out(u, gr):
            turned = tile_of("turned_o%d" % gr, u, [P, UNIT, 4], BF16)
            words = tiles["short%d" % gr, u][:].rearrange("p s e q v -> p (s e q v)").bitcast(F32)
            bank = psum.tile([P, 2, UNIT], F32, name="bank_p", tag="tp", bufs=3)
            for rt in range(RT):
                for e in range(2):
                    first = 256 * rt + P * e
                    nc.tensor.transpose(bank[:, e, P * rt : P * (rt + 1)], words[:, first : first + P], ident[:])
            bank_to_words(bank, turned[:])

        def quantize_out(u, gr):
            codes = tile_of("codes_o", u, [P, GROUPS, UNIT], U32)
            scales = tile_of("scales_o", u, [P, GROUPS, UNIT], U8)
            nc.vector.quantize_mx(
                out=codes[:, gr, :].bitcast(FP8X4),
                scales=scales[:, gr, :],
                in_=tiles["turned_o%d" % gr, u][:].rearrange("p r j -> p (r j)"),
            )
            if gr == GROUPS - 1:
                cols = slice(UNIT * u, UNIT * (u + 1))
                nc.sync.dma_start(
                    out=out_1[:, :, cols, :].rearrange("g p m t -> p g (m t)").bitcast(I32), in_=codes[:].bitcast(I32)
                )
                for q in range(4):
                    nc.sync.dma_start(
                        out=out_2[:, 4 * q : 4 * q + 4, cols].bitcast(I32).rearrange("g r m -> r g m"),
                        in_=scales[32 * q : 32 * q + 4].rearrange("r g m -> r (g m)").bitcast(I32).rearrange("r (g m) -> r g m", g=GROUPS),
                    )

        steps = {
            "phi_words_of": phi_words_of,
            "phi_scales_of": phi_scales_of,
            "warm_up": warm_up,
            "turn_z": turn_z,
            "turn_x": turn_x,
            "quantize_z": quantize_z,
            "quantize_x": quantize_x,
            "turn_g": turn_g,
            "z_bank": z_bank,
            "pair_squares": pair_squares,
            "sum_squares": sum_squares,
            "invert": invert,
            "numerator": numerator,
            "ridge": ridge,
            "x_bank": x_bank,
            "quantize_y": quantize_y,
            "out_bank": out_bank,
            "round_bank": round_bank,
            "turn_out": turn_out,
            "quantize_out": quantize_out,
        }
        last = max(behind for step, i, behind in SLOT)
        for slot in range(UNITS + last):
            for step, i, behind in SLOT:
                if 0 <= slot - behind < UNITS:
                    steps[step](slot - behind, i)
